import numpy as np
import ml_dtypes


def mxq(x, axis, fmt="e4m3"):
    dtype, down = {"e4m3": (ml_dtypes.float8_e4m3fn, 7), "e5m2": (ml_dtypes.float8_e5m2, 14)}[fmt]
    v = np.moveaxis(np.asarray(x, np.float32).astype(ml_dtypes.bfloat16).astype(np.float64), axis, -1)
    blocks = v.reshape(v.shape[:-1] + (-1, 32))
    amax = np.abs(blocks).max(-1, keepdims=True)
    byte = np.maximum(np.where(amax > 0, np.frexp(amax)[1] - 1 + 127, 0) - down, 1)
    scale = np.exp2(byte - 127.0)
    codes = (blocks / scale).astype(np.float32).astype(dtype).astype(np.float64)
    return np.moveaxis((codes * scale).reshape(v.shape), -1, axis)


WIDE = False


def mx_kscale(k):
    if not WIDE:
        return np.ones(k)
    levels = np.array([10, -10, 5, -5, 0])
    if k % 512:
        return np.exp2(np.random.permutation(np.resize(levels, k // 32))).repeat(32)
    a = np.empty((k // 512, 16))
    for p in range(k // 512):
        a[p, :8] = np.random.permutation(np.resize(levels, 8))
        for g in range(8):
            far = levels[np.abs(levels - a[p, g]) >= 10]
            a[p, g + 8] = far[np.random.randint(len(far))]
    return np.exp2(a.ravel()).repeat(32)


def f64(x):
    return np.asarray(x).astype(np.float64)


def striped(idx):
    return np.tile(idx.reshape(-1, 16).T, (8, 1)).astype(np.uint16)


def unstriped(offs):
    return offs[:16].T.reshape(-1).astype(np.int64)


def striped8(idx):
    return np.concatenate([x.reshape(-1, 16).T for x in idx]).astype(np.uint16)


def runs(offs, k):
    lists = np.stack([offs[16 * r : 16 * r + 16].T.reshape(-1) for r in range(8)]).astype(np.int64)
    return lists[np.arange(k) % 512 // 64]


def pack_weight(w):
    k, n = w.shape
    w = f64(np.asarray(w, np.float32).astype(ml_dtypes.bfloat16)).reshape(k // 32, 32, n)
    amax = np.abs(w).max(1)
    byte = np.clip(np.where(amax > 0, np.frexp(amax)[1] - 1 + 127 - 7, 1), 1, 254)
    scaled = (w * np.exp2(127.0 - byte)[:, None, :]).reshape(k, n).astype(np.float32)
    words = np.ascontiguousarray(scaled.reshape(k // 512, 128, 4, n).transpose(0, 1, 3, 2)).astype(ml_dtypes.float8_e4m3fn).view(np.uint8)
    return words, np.ascontiguousarray(byte.astype(np.uint8).reshape(k // 512, 16, n))


def unpack_weight(words, scales):
    g, p, n, _ = words.shape
    vals = np.ascontiguousarray(words).view(ml_dtypes.float8_e4m3fn).astype(np.float64) * np.repeat(np.exp2(scales.astype(np.float64) - 127.0), 8, axis=1)[..., None]
    return vals.transpose(0, 1, 3, 2).reshape(g * 512, n)


K, T, S, H, G, W = 512, 1024, 256, 512, 2048, 128


def setup_inputs():
    n = np.random.standard_normal
    s = mx_kscale(K)[:, None]
    packed_xT = pack_weight(n((K, T)) * s)
    packed_dT = pack_weight(n((K, G)) / s)
    perm = np.random.permutation(S)
    return {
        "x_words": packed_xT[0],
        "x_scales": packed_xT[1],
        "w1": (n((K, H)) / np.sqrt(K) / s).astype(np.float32),
        "gs": (np.random.uniform(0.5, 1.5, (K, 1)) * s).astype(np.float32),
        "d_words": packed_dT[0],
        "d_scales": packed_dT[1],
        "offs": striped(np.random.permutation(T)[:S]),
        "k1": striped8(np.random.randint(0, G, (8, H))),
        "k2": striped8(np.random.randint(0, G, (8, H))),
        "hz": striped8(np.random.randint(0, T, (8, S))),
        "n1": striped(perm[:W]),
        "n2": striped(perm[W:]),
        "n3": striped(np.random.permutation(S)),
    }


def reference(x_words, x_scales, w1, gs, d_words, d_scales, offs, k1, k2, hz, n1, n2, n3):
    d_k1 = unpack_weight(d_words, d_scales)[np.arange(K)[:, None], runs(k1, K)]
    xq = unpack_weight(x_words, x_scales)[:, unstriped(offs)]
    y = mxq(f64(w1), 0, "e4m3").T @ xq
    z = f64(gs) * y
    d_k2 = unpack_weight(d_words, d_scales)[np.arange(K)[:, None], runs(k2, K)]
    x_hz = unpack_weight(x_words, x_scales)[np.arange(K)[:, None], runs(hz, K)]
    h = 0.0625 * ((d_k1.T @ mxq(z, 0, "e4m3") + d_k2.T @ x_hz))
    pa = h[:, unstriped(n1)]
    pb = h[:, unstriped(n2)]
    rb = pa - pb
    ds = np.zeros((H, S))
    ds[:, unstriped(n1)] = pb
    dt = ds.copy()
    dt[:, unstriped(n2)] = rb
    return np.maximum(dt, 0.5 * dt[:, unstriped(n3)])

@@ -1,0 +1,205 @@
+from contextlib import ExitStack
+
+import concourse.mybir as mybir
+
+K, T, S, H, G, W = 512, 1024, 256, 512, 2048, 128
+FLOPS = 3 * 2 * K * H * S
+
+F32 = mybir.dt.float32
+BF16 = mybir.dt.bfloat16
+I32 = mybir.dt.int32
+U32 = mybir.dt.uint32
+U16 = mybir.dt.uint16
+U8 = mybir.dt.uint8
+FP8X4 = mybir.dt.float8_e4m3fn_x4
+COPY = mybir.ActivationFunctionType.Copy
+ALU = mybir.AluOpType
+
+P = 128
+PACK = 4
+HALF = 256
+LIST_ROWS = 16
+
+
+def tile_picked_cmixhiswapd_none_p_kernel(
+    tc, x_words, x_scales, w1, gs, d_words, d_scales, offs, k1, k2, hz, n1, n2, n3, out
+):
+    nc = tc.nc
+    with ExitStack() as ctx:
+        keep = ctx.enter_context(tc.tile_pool(name="keep", bufs=1))
+        psum = ctx.enter_context(tc.psum_pool(name="psum", bufs=1))
+
+        def sb(name, shape, dtype, tag=None):
+            return keep.tile(shape, dtype, name=name, tag=tag or name, align_bytes=64)
+
+        def load_list(name, src):
+            lst = keep.tile([P, src.shape[1]], U16, name=name, tag=name)
+            nc.sync.dma_start(lst[:], src)
+            return lst
+
+        def load_scales(table, src):
+            nc.sync.dma_start(table[:].bitcast(I32)[0:P:8, :], src[0].bitcast(I32))
+
+        def load_words(name, src):
+            table = sb(name, [P, src.shape[2]], U32)
+            nc.scalar.dma_start(table[:].bitcast(I32), src[0].rearrange("p n t -> p (n t)").bitcast(I32))
+            return table
+
+        def gather(dst, table, lst, first, count):
+            nc.vector.tensor_copy(dst, table[:].indirect(lst[:, first // LIST_ROWS : (first + count) // LIST_ROWS]))
+
+        def place_scales(plane, picked):
+            for q in range(4):
+                nc.sync.dma_start(
+                    plane[:].bitcast(I32)[32 * q : 32 * q + 4, :], picked[:].bitcast(I32)[32 * q : 32 * q + 32 : 8, :]
+                )
+
+        xs = sb("xs", [P, T], U8)
+        ds = sb("ds", [P, G], U8)
+        plane_a = sb("plane_a", [P, 4 * HALF], U8)
+        plane_b = sb("plane_b", [P, 2 * HALF], U8)
+        for zeroed in (xs, ds, plane_a, plane_b):
+            nc.vector.memset(zeroed[:].bitcast(I32), 0)
+
+        offs_l = load_list("offs_l", offs)
+        load_scales(xs, x_scales)
+        hz_l = load_list("hz_l", hz)
+        load_scales(ds, d_scales)
+        k2_l = load_list("k2_l", k2)
+        k1_l = load_list("k1_l", k1)
+        n2_l = load_list("n2_l", n2)
+        n1_l = load_list("n1_l", n1)
+        n3_l = load_list("n3_l", n3)
+        w_rows = w1.rearrange("(p j) c -> p j c", j=PACK)
+        w_raw = []
+        for u in range(2):
+            part = sb("w_raw%d" % u, [P, PACK, HALF], F32)
+            nc.scalar.dma_start(part[:], w_rows[:, :, u * HALF : (u + 1) * HALF])
+            w_raw.append(part)
+        xw = load_words("xw", x_words)
+        gain = sb("gain", [P, PACK], F32)
+        nc.gpsimd.dma_start(gain[:], gs.rearrange("(p t) o -> p (t o)", t=PACK))
+
+        bytes_a = sb("bytes_a", [P, 4 * HALF], U8)
+        gather(bytes_a[:, 3 * HALF : 4 * HALF], xs, offs_l, 0, S)
+        gather(bytes_a[:, 0:HALF], xs, hz_l, 0, S)
+        gather(bytes_a[:, HALF : 2 * HALF], ds, k2_l, 0, HALF)
+        gather(bytes_a[:, 2 * HALF : 3 * HALF], ds, k1_l, 0, HALF)
+        place_scales(plane_a, bytes_a)
+
+        w_bf = sb("w_bf", [P, PACK, P, PACK], BF16)
+
+        def round_weights(u):
+            nc.scalar.activation(
+                w_bf[:, :, 64 * u : 64 * (u + 1), :].rearrange("p t m j -> p m t j"),
+                w_raw[u][:].rearrange("p j (m t) -> p m t j", t=PACK),
+                COPY,
+            )
+
+        round_weights(0)
+        dw = load_words("dw", d_words)
+        round_weights(1)
+        w_codes = sb("w_codes", [P, H], U32)
+        w_plane = sb("w_plane", [P, H], U8)
+        nc.vector.quantize_mx(w_codes[:].bitcast(FP8X4), w_plane[:], w_bf[:].rearrange("p t m j -> p (t m j)"))
+
+        xq = sb("xq", [P, S], U32)
+        gather(xq[:], xw, offs_l, 0, S)
+        xh = sb("xh", [P, S], U32)
+        gather(xh[:], xw, hz_l, 0, S)
+
+        z_codes = sb("z_codes", [P, S], U32)
+        z_plane = sb("z_plane", [P, S], U8)
+        z_bf = []
+        for u in range(2):
+            y = psum.tile([P, PACK, P], F32, name="y%d" % u, tag="y%d" % u)
+            cols = slice(u * P, (u + 1) * P)
+            for t in range(PACK):
+                rows = slice(t * P, (t + 1) * P)
+                nc.tensor.matmul_mx(
+                    y[:, t, :],
+                    lhsT=w_codes[:, rows].bitcast(FP8X4),
+                    lhsT_scale=w_plane[:, rows],
+                    rhs=xq[:, cols].bitcast(FP8X4),
+                    rhs_scale=plane_a[:, 3 * HALF + u * P : 3 * HALF + (u + 1) * P],
+                    start=True,
+                    stop=True,
+                )
+            z = sb("z_bf%d" % u, [P, P, PACK], BF16)
+            nc.vector.tensor_tensor(
+                z[:], y[:].rearrange("p t c -> p c t"), gain[:].unsqueeze(1).to_broadcast([P, P, PACK]), ALU.mult
+            )
+            z_bf.append(z)
+
+        words_a = sb("words_a", [P, 2 * HALF], U32)
+        gather(words_a[:, 0:HALF], dw, k2_l, 0, HALF)
+        gather(words_a[:, HALF : 2 * HALF], dw, k1_l, 0, HALF)
+
+        for u in range(2):
+            cols = slice(u * P, (u + 1) * P)
+            nc.vector.quantize_mx(
+                z_codes[:, cols].bitcast(FP8X4), z_plane[:, cols], z_bf[u][:].rearrange("p c t -> p (c t)")
+            )
+
+        def product(i, words, plane, base):
+            acc = psum.tile([P, S], F32, name="acc%d" % i, tag="acc%d" % i)
+            m0 = (i % 2) * P
+            nc.tensor.matmul_mx(
+                acc[:],
+                lhsT=words[:, m0 : m0 + P].bitcast(FP8X4),
+                lhsT_scale=plane[:, base + m0 : base + m0 + P],
+                rhs=xh[:].bitcast(FP8X4),
+                rhs_scale=plane_a[:, 0:S],
+                start=True,
+                stop=False,
+            )
+            nc.tensor.matmul_mx(
+                acc[:],
+                lhsT=words[:, HALF + m0 : HALF + m0 + P].bitcast(FP8X4),
+                lhsT_scale=plane[:, base + HALF + m0 : base + HALF + m0 + P],
+                rhs=z_codes[:].bitcast(FP8X4),
+                rhs_scale=z_plane[:],
+                start=False,
+                stop=True,
+            )
+            h = sb("h%d" % i, [P, S], F32)
+            if i == 0:
+                nc.scalar.activation(h[:], acc[:], COPY, scale=0.0625)
+            else:
+                nc.vector.tensor_scalar_mul(h[:], acc[:], 0.0625)
+            return h
+
+        def swap(i, h):
+            pa = sb("pa%d" % i, [P, W], F32)
+            pb = sb("pb%d" % i, [P, W], F32)
+            rb = sb("rb%d" % i, [P, W], F32)
+            dt = sb("dt%d" % i, [P, S], F32)
+            nc.scalar.activation(pb[:], h[:].indirect(n2_l[:]), COPY)
+            nc.scalar.activation(pa[:], h[:].indirect(n1_l[:]), COPY)
+            nc.vector.tensor_tensor(rb[:], pa[:], pb[:], ALU.subtract)
+            nc.scalar.activation(dt[:].indirect(n1_l[:]), pb[:], COPY)
+            nc.scalar.activation(dt[:].indirect(n2_l[:]), rb[:], COPY)
+            return dt
+
+        def finish(i, dt):
+            far = sb("far%d" % i, [P, S], F32)
+            res = sb("res%d" % i, [P, S], F32)
+            for u in range(2):
+                nc.scalar.activation(far[:, u * W : (u + 1) * W], dt[:].indirect(n3_l[:, 8 * u : 8 * (u + 1)]), COPY)
+            nc.vector.scalar_tensor_tensor(res[:], far[:], 0.5, dt[:], ALU.mult, ALU.max)
+            nc.sync.dma_start(out[i * P : (i + 1) * P, :], res[:])
+
+        hs = [product(i, words_a, plane_a, HALF) for i in range(2)]
+
+        bytes_b = sb("bytes_b", [P, 2 * HALF], U8, tag="z_bf0")
+        gather(bytes_b[:, 0:HALF], ds, k2_l, HALF, HALF)
+        gather(bytes_b[:, HALF : 2 * HALF], ds, k1_l, HALF, HALF)
+        place_scales(plane_b, bytes_b)
+        words_b = sb("words_b", [P, 2 * HALF], U32, tag="z_bf1")
+        gather(words_b[:, 0:HALF], dw, k2_l, HALF, HALF)
+        gather(words_b[:, HALF : 2 * HALF], dw, k1_l, HALF, HALF)
+
+        for i in range(2):
+            finish(i, swap(i, hs[i]))
+        for i in range(2, 4):
+            finish(i, swap(i, product(i, words_b, plane_b, 0)))

@@ -19,6 +19,9 @@ P = 128
 PACK = 4
 HALF = 256
 LIST_ROWS = 16
+EARLY = 512
+SPARE = 16
+W_SPLIT = 48
 
 
 def tile_picked_cmixhiswapd_none_p_kernel(
@@ -40,76 +43,82 @@ def tile_picked_cmixhiswapd_none_p_kernel(
         def load_scales(table, src):
             nc.sync.dma_start(table[:].bitcast(I32)[0:P:8, :], src[0].bitcast(I32))
 
-        def load_words(name, src):
-            table = sb(name, [P, src.shape[2]], U32)
-            nc.scalar.dma_start(table[:].bitcast(I32), src[0].rearrange("p n t -> p (n t)").bitcast(I32))
-            return table
+        def load_words(table, src, first, last):
+            words = src[0].rearrange("p n t -> p (n t)").bitcast(I32)
+            nc.sync.dma_start(table[:].bitcast(I32)[:, first:last], words[:, first:last])
 
         def gather(dst, table, lst, first, count):
             nc.vector.tensor_copy(dst, table[:].indirect(lst[:, first // LIST_ROWS : (first + count) // LIST_ROWS]))
 
-        def place_scales(plane, picked):
+        def place_scales(queue, plane, picked):
             for q in range(4):
-                nc.sync.dma_start(
+                queue.dma_start(
                     plane[:].bitcast(I32)[32 * q : 32 * q + 4, :], picked[:].bitcast(I32)[32 * q : 32 * q + 32 : 8, :]
                 )
 
         xs = sb("xs", [P, T], U8)
         ds = sb("ds", [P, G], U8)
-        plane_a = sb("plane_a", [P, 4 * HALF], U8)
+        plane_x = sb("plane_x", [P, S], U8)
+        plane_a = sb("plane_a", [P, 3 * HALF], U8)
         plane_b = sb("plane_b", [P, 2 * HALF], U8)
-        for zeroed in (xs, ds, plane_a, plane_b):
+        nc.vector.memset(ds[:, 0 : G // 2].bitcast(I32), 0)
+        nc.gpsimd.memset(ds[:, G // 2 : G].bitcast(I32), 0)
+        for zeroed in (plane_a, plane_b):
             nc.vector.memset(zeroed[:].bitcast(I32), 0)
+        dts = [sb("dt%d" % i, [P, S + SPARE], F32) for i in range(4)]
+        for dt in dts:
+            nc.vector.memset(dt[:, S:], 0.0)
 
         offs_l = load_list("offs_l", offs)
-        load_scales(xs, x_scales)
+        x_rows = x_scales[0].bitcast(I32)
+        nc.sync.dma_start(xs[:].bitcast(I32), x_rows.unsqueeze(1).to_broadcast([16, 8, T // 4]))
         hz_l = load_list("hz_l", hz)
-        load_scales(ds, d_scales)
         k2_l = load_list("k2_l", k2)
         k1_l = load_list("k1_l", k1)
+        load_scales(ds, d_scales)
+        w_rows = w1.rearrange("(p j) c -> p j c", j=PACK)
         n2_l = load_list("n2_l", n2)
+        w_raw = sb("w_raw", [P, PACK, H], F32)
+        nc.sync.dma_start(w_raw[:], w_rows)
+        xw = sb("xw", [P, T], U32)
+        load_words(xw, x_words, 0, T)
         n1_l = load_list("n1_l", n1)
         n3_l = load_list("n3_l", n3)
-        w_rows = w1.rearrange("(p j) c -> p j c", j=PACK)
-        w_raw = []
-        for u in range(2):
-            part = sb("w_raw%d" % u, [P, PACK, HALF], F32)
-            nc.scalar.dma_start(part[:], w_rows[:, :, u * HALF : (u + 1) * HALF])
-            w_raw.append(part)
-        xw = load_words("xw", x_words)
-        gain = sb("gain", [P, PACK], F32)
-        nc.gpsimd.dma_start(gain[:], gs.rearrange("(p t) o -> p (t o)", t=PACK))
 
-        bytes_a = sb("bytes_a", [P, 4 * HALF], U8)
-        gather(bytes_a[:, 3 * HALF : 4 * HALF], xs, offs_l, 0, S)
+        bytes_x = sb("bytes_x", [P, S], U8)
+        gather(bytes_x[:], xs, offs_l, 0, S)
+        nc.vector.tensor_copy(plane_x[:].bitcast(I32), bytes_x[:].bitcast(I32))
+        for r in range(1, 4):
+            nc.sync.dma_start(plane_x[:].bitcast(I32)[r:P:32, :], plane_x[:].bitcast(I32)[8 * r : P : 32, :])
+        bytes_a = sb("bytes_a", [P, 3 * HALF], U8, tag="bytes_x")
         gather(bytes_a[:, 0:HALF], xs, hz_l, 0, S)
+        dw = sb("dw", [P, G], U32, tag="xs")
+        load_words(dw, d_words, 0, G)
         gather(bytes_a[:, HALF : 2 * HALF], ds, k2_l, 0, HALF)
         gather(bytes_a[:, 2 * HALF : 3 * HALF], ds, k1_l, 0, HALF)
-        place_scales(plane_a, bytes_a)
+        place_scales(nc.sync, plane_a, bytes_a)
 
         w_bf = sb("w_bf", [P, PACK, P, PACK], BF16)
 
-        def round_weights(u):
-            nc.scalar.activation(
-                w_bf[:, :, 64 * u : 64 * (u + 1), :].rearrange("p t m j -> p m t j"),
-                w_raw[u][:].rearrange("p j (m t) -> p m t j", t=PACK),
-                COPY,
+        def dealt(first, last):
+            return (
+                w_bf[:, :, first:last, :].rearrange("p t m j -> p m t j"),
+                w_raw[:, :, PACK * first : PACK * last].rearrange("p j (m t) -> p m t j", t=PACK),
             )
 
-        round_weights(0)
-        dw = load_words("dw", d_words)
-        round_weights(1)
+        nc.scalar.activation(*dealt(0, W_SPLIT), COPY)
+        nc.vector.tensor_copy(*dealt(W_SPLIT, P))
+        gain = sb("gain", [P, PACK], F32)
+        nc.gpsimd.dma_start(gain[:], gs.rearrange("(p t) o -> p (t o)", t=PACK))
         w_codes = sb("w_codes", [P, H], U32)
         w_plane = sb("w_plane", [P, H], U8)
         nc.vector.quantize_mx(w_codes[:].bitcast(FP8X4), w_plane[:], w_bf[:].rearrange("p t m j -> p (t m j)"))
 
         xq = sb("xq", [P, S], U32)
         gather(xq[:], xw, offs_l, 0, S)
-        xh = sb("xh", [P, S], U32)
+        xh = sb("xh", [P, S], U32, tag="w_bf")
         gather(xh[:], xw, hz_l, 0, S)
 
-        z_codes = sb("z_codes", [P, S], U32)
-        z_plane = sb("z_plane", [P, S], U8)
         z_bf = []
         for u in range(2):
             y = psum.tile([P, PACK, P], F32, name="y%d" % u, tag="y%d" % u)
@@ -121,20 +130,28 @@ def tile_picked_cmixhiswapd_none_p_kernel(
                     lhsT=w_codes[:, rows].bitcast(FP8X4),
                     lhsT_scale=w_plane[:, rows],
                     rhs=xq[:, cols].bitcast(FP8X4),
-                    rhs_scale=plane_a[:, 3 * HALF + u * P : 3 * HALF + (u + 1) * P],
+                    rhs_scale=plane_x[:, cols],
                     start=True,
                     stop=True,
                 )
-            z = sb("z_bf%d" % u, [P, P, PACK], BF16)
-            nc.vector.tensor_tensor(
-                z[:], y[:].rearrange("p t c -> p c t"), gain[:].unsqueeze(1).to_broadcast([P, P, PACK]), ALU.mult
-            )
+            z = sb("z_bf%d" % u, [P, P, PACK], BF16, tag="bytes_x" if u == 1 else None)
+            if u == 0:
+                z_rows = sb("z_rows", [P, PACK, P], BF16)
+                for t in range(PACK):
+                    nc.scalar.activation(z_rows[:, t, :], y[:, t, :], COPY, scale=gain[:, t : t + 1])
+                nc.scalar.copy(z[:], z_rows[:].rearrange("p t c -> p c t"))
+            else:
+                nc.vector.tensor_tensor(
+                    z[:], y[:].rearrange("p t c -> p c t"), gain[:].unsqueeze(1).to_broadcast([P, P, PACK]), ALU.mult
+                )
             z_bf.append(z)
 
         words_a = sb("words_a", [P, 2 * HALF], U32)
         gather(words_a[:, 0:HALF], dw, k2_l, 0, HALF)
         gather(words_a[:, HALF : 2 * HALF], dw, k1_l, 0, HALF)
 
+        z_codes = sb("z_codes", [P, S], U32, tag="gain")
+        z_plane = sb("z_plane", [P, S], U8)
         for u in range(2):
             cols = slice(u * P, (u + 1) * P)
             nc.vector.quantize_mx(
@@ -173,7 +190,7 @@ def tile_picked_cmixhiswapd_none_p_kernel(
             pa = sb("pa%d" % i, [P, W], F32)
             pb = sb("pb%d" % i, [P, W], F32)
             rb = sb("rb%d" % i, [P, W], F32)
-            dt = sb("dt%d" % i, [P, S], F32)
+            dt = dts[i]
             nc.scalar.activation(pb[:], h[:].indirect(n2_l[:]), COPY)
             nc.scalar.activation(pa[:], h[:].indirect(n1_l[:]), COPY)
             nc.vector.tensor_tensor(rb[:], pa[:], pb[:], ALU.subtract)
@@ -181,25 +198,34 @@ def tile_picked_cmixhiswapd_none_p_kernel(
             nc.scalar.activation(dt[:].indirect(n2_l[:]), rb[:], COPY)
             return dt
 
-        def finish(i, dt):
-            far = sb("far%d" % i, [P, S], F32)
-            res = sb("res%d" % i, [P, S], F32)
-            for u in range(2):
-                nc.scalar.activation(far[:, u * W : (u + 1) * W], dt[:].indirect(n3_l[:, 8 * u : 8 * (u + 1)]), COPY)
-            nc.vector.scalar_tensor_tensor(res[:], far[:], 0.5, dt[:], ALU.mult, ALU.max)
+        def finish(i, dt, far_tag=None, res_tag=None):
+            far = sb("far%d" % i, [P, S], F32, tag=far_tag)
+            res = sb("res%d" % i, [P, S], F32, tag=res_tag)
+            nc.scalar.activation(far[:], dt[:].indirect(n3_l[:]), COPY)
+            nc.vector.scalar_tensor_tensor(res[:], far[:], 0.5, dt[:, 0:S], ALU.mult, ALU.max)
             nc.sync.dma_start(out[i * P : (i + 1) * P, :], res[:])
 
         hs = [product(i, words_a, plane_a, HALF) for i in range(2)]
 
-        bytes_b = sb("bytes_b", [P, 2 * HALF], U8, tag="z_bf0")
+        bytes_b = sb("bytes_b", [P, 2 * HALF], U8, tag="bytes_x")
         gather(bytes_b[:, 0:HALF], ds, k2_l, HALF, HALF)
         gather(bytes_b[:, HALF : 2 * HALF], ds, k1_l, HALF, HALF)
-        place_scales(plane_b, bytes_b)
-        words_b = sb("words_b", [P, 2 * HALF], U32, tag="z_bf1")
+        place_scales(nc.sync, plane_b, bytes_b)
+        dt0 = swap(0, hs[0])
+        words_b = sb("words_b", [P, 2 * HALF], U32, tag="pa0")
         gather(words_b[:, 0:HALF], dw, k2_l, HALF, HALF)
         gather(words_b[:, HALF : 2 * HALF], dw, k1_l, HALF, HALF)
-
-        for i in range(2):
-            finish(i, swap(i, hs[i]))
-        for i in range(2, 4):
-            finish(i, swap(i, product(i, words_b, plane_b, 0)))
+        dt1 = swap(1, hs[1])
+        hs.extend([product(i, words_b, plane_b, 0) for i in range(2, 4)])
+        dt2 = swap(2, hs[2])
+        finish(0, dt0, res_tag="pa0")
+        finish(1, dt1, far_tag="plane_b")
+        dt3 = swap(3, hs[3])
+        finish(2, dt2)
+        far = sb("far3", [P, S], F32)
+        res = sb("res3", [P, S], F32)
+        for u in range(2):
+            cols = slice(u * W, (u + 1) * W)
+            nc.scalar.activation(far[:, cols], dt3[:].indirect(n3_l[:, 8 * u : 8 * (u + 1)]), COPY)
+            nc.vector.scalar_tensor_tensor(res[:, cols], far[:, cols], 0.5, dt3[:, cols], ALU.mult, ALU.max)
+            nc.sync.dma_start(out[3 * P : 4 * P, cols], res[:, cols])

from contextlib import ExitStack

import concourse.mybir as mybir

K, T, S, H, G, W = 512, 1024, 256, 512, 2048, 128
FLOPS = 3 * 2 * K * H * S

F32 = mybir.dt.float32
BF16 = mybir.dt.bfloat16
I32 = mybir.dt.int32
U32 = mybir.dt.uint32
U16 = mybir.dt.uint16
U8 = mybir.dt.uint8
FP8X4 = mybir.dt.float8_e4m3fn_x4
COPY = mybir.ActivationFunctionType.Copy
ALU = mybir.AluOpType

P = 128
PACK = 4
HALF = 256
LIST_ROWS = 16
EARLY = 512
SPARE = 16
W_SPLIT = 48


def tile_picked_cmixhiswapd_none_p_kernel(
    tc, x_words, x_scales, w1, gs, d_words, d_scales, offs, k1, k2, hz, n1, n2, n3, out
):
    nc = tc.nc
    with ExitStack() as ctx:
        keep = ctx.enter_context(tc.tile_pool(name="keep", bufs=1))
        psum = ctx.enter_context(tc.psum_pool(name="psum", bufs=1))

        def sb(name, shape, dtype, tag=None):
            return keep.tile(shape, dtype, name=name, tag=tag or name, align_bytes=64)

        def load_list(name, src):
            lst = keep.tile([P, src.shape[1]], U16, name=name, tag=name)
            nc.sync.dma_start(lst[:], src)
            return lst

        def load_scales(table, src):
            nc.sync.dma_start(table[:].bitcast(I32)[0:P:8, :], src[0].bitcast(I32))

        def load_words(table, src, first, last):
            words = src[0].rearrange("p n t -> p (n t)").bitcast(I32)
            nc.sync.dma_start(table[:].bitcast(I32)[:, first:last], words[:, first:last])

        def gather(dst, table, lst, first, count):
            nc.vector.tensor_copy(dst, table[:].indirect(lst[:, first // LIST_ROWS : (first + count) // LIST_ROWS]))

        def place_scales(queue, plane, picked):
            for q in range(4):
                queue.dma_start(
                    plane[:].bitcast(I32)[32 * q : 32 * q + 4, :], picked[:].bitcast(I32)[32 * q : 32 * q + 32 : 8, :]
                )

        xs = sb("xs", [P, T], U8)
        ds = sb("ds", [P, G], U8)
        plane_x = sb("plane_x", [P, S], U8)
        plane_a = sb("plane_a", [P, 3 * HALF], U8)
        plane_b = sb("plane_b", [P, 2 * HALF], U8)
        nc.vector.memset(ds[:, 0 : G // 2].bitcast(I32), 0)
        nc.gpsimd.memset(ds[:, G // 2 : G].bitcast(I32), 0)
        for zeroed in (plane_a, plane_b):
            nc.vector.memset(zeroed[:].bitcast(I32), 0)
        dts = [sb("dt%d" % i, [P, S + SPARE], F32) for i in range(4)]
        for dt in dts:
            nc.vector.memset(dt[:, S:], 0.0)

        offs_l = load_list("offs_l", offs)
        x_rows = x_scales[0].bitcast(I32)
        nc.sync.dma_start(xs[:].bitcast(I32), x_rows.unsqueeze(1).to_broadcast([16, 8, T // 4]))
        hz_l = load_list("hz_l", hz)
        k2_l = load_list("k2_l", k2)
        k1_l = load_list("k1_l", k1)
        load_scales(ds, d_scales)
        w_rows = w1.rearrange("(p j) c -> p j c", j=PACK)
        n2_l = load_list("n2_l", n2)
        w_raw = sb("w_raw", [P, PACK, H], F32)
        nc.sync.dma_start(w_raw[:], w_rows)
        xw = sb("xw", [P, T], U32)
        load_words(xw, x_words, 0, T)
        n1_l = load_list("n1_l", n1)
        n3_l = load_list("n3_l", n3)

        bytes_x = sb("bytes_x", [P, S], U8)
        gather(bytes_x[:], xs, offs_l, 0, S)
        nc.vector.tensor_copy(plane_x[:].bitcast(I32), bytes_x[:].bitcast(I32))
        for r in range(1, 4):
            nc.sync.dma_start(plane_x[:].bitcast(I32)[r:P:32, :], plane_x[:].bitcast(I32)[8 * r : P : 32, :])
        bytes_a = sb("bytes_a", [P, 3 * HALF], U8, tag="bytes_x")
        gather(bytes_a[:, 0:HALF], xs, hz_l, 0, S)
        dw = sb("dw", [P, G], U32, tag="xs")
        load_words(dw, d_words, 0, G)
        gather(bytes_a[:, HALF : 2 * HALF], ds, k2_l, 0, HALF)
        gather(bytes_a[:, 2 * HALF : 3 * HALF], ds, k1_l, 0, HALF)
        place_scales(nc.sync, plane_a, bytes_a)

        w_bf = sb("w_bf", [P, PACK, P, PACK], BF16)

        def dealt(first, last):
            return (
                w_bf[:, :, first:last, :].rearrange("p t m j -> p m t j"),
                w_raw[:, :, PACK * first : PACK * last].rearrange("p j (m t) -> p m t j", t=PACK),
            )

        nc.scalar.activation(*dealt(0, W_SPLIT), COPY)
        nc.vector.tensor_copy(*dealt(W_SPLIT, P))
        gain = sb("gain", [P, PACK], F32)
        nc.gpsimd.dma_start(gain[:], gs.rearrange("(p t) o -> p (t o)", t=PACK))
        w_codes = sb("w_codes", [P, H], U32)
        w_plane = sb("w_plane", [P, H], U8)
        nc.vector.quantize_mx(w_codes[:].bitcast(FP8X4), w_plane[:], w_bf[:].rearrange("p t m j -> p (t m j)"))

        xq = sb("xq", [P, S], U32)
        gather(xq[:], xw, offs_l, 0, S)
        xh = sb("xh", [P, S], U32, tag="w_bf")
        gather(xh[:], xw, hz_l, 0, S)

        z_bf = []
        for u in range(2):
            y = psum.tile([P, PACK, P], F32, name="y%d" % u, tag="y%d" % u)
            cols = slice(u * P, (u + 1) * P)
            for t in range(PACK):
                rows = slice(t * P, (t + 1) * P)
                nc.tensor.matmul_mx(
                    y[:, t, :],
                    lhsT=w_codes[:, rows].bitcast(FP8X4),
                    lhsT_scale=w_plane[:, rows],
                    rhs=xq[:, cols].bitcast(FP8X4),
                    rhs_scale=plane_x[:, cols],
                    start=True,
                    stop=True,
                )
            z = sb("z_bf%d" % u, [P, P, PACK], BF16, tag="bytes_x" if u == 1 else None)
            if u == 0:
                z_rows = sb("z_rows", [P, PACK, P], BF16)
                for t in range(PACK):
                    nc.scalar.activation(z_rows[:, t, :], y[:, t, :], COPY, scale=gain[:, t : t + 1])
                nc.scalar.copy(z[:], z_rows[:].rearrange("p t c -> p c t"))
            else:
                nc.vector.tensor_tensor(
                    z[:], y[:].rearrange("p t c -> p c t"), gain[:].unsqueeze(1).to_broadcast([P, P, PACK]), ALU.mult
                )
            z_bf.append(z)

        words_a = sb("words_a", [P, 2 * HALF], U32)
        gather(words_a[:, 0:HALF], dw, k2_l, 0, HALF)
        gather(words_a[:, HALF : 2 * HALF], dw, k1_l, 0, HALF)

        z_codes = sb("z_codes", [P, S], U32, tag="gain")
        z_plane = sb("z_plane", [P, S], U8)
        for u in range(2):
            cols = slice(u * P, (u + 1) * P)
            nc.vector.quantize_mx(
                z_codes[:, cols].bitcast(FP8X4), z_plane[:, cols], z_bf[u][:].rearrange("p c t -> p (c t)")
            )

        def product(i, words, plane, base):
            acc = psum.tile([P, S], F32, name="acc%d" % i, tag="acc%d" % i)
            m0 = (i % 2) * P
            nc.tensor.matmul_mx(
                acc[:],
                lhsT=words[:, m0 : m0 + P].bitcast(FP8X4),
                lhsT_scale=plane[:, base + m0 : base + m0 + P],
                rhs=xh[:].bitcast(FP8X4),
                rhs_scale=plane_a[:, 0:S],
                start=True,
                stop=False,
            )
            nc.tensor.matmul_mx(
                acc[:],
                lhsT=words[:, HALF + m0 : HALF + m0 + P].bitcast(FP8X4),
                lhsT_scale=plane[:, base + HALF + m0 : base + HALF + m0 + P],
                rhs=z_codes[:].bitcast(FP8X4),
                rhs_scale=z_plane[:],
                start=False,
                stop=True,
            )
            h = sb("h%d" % i, [P, S], F32)
            if i == 0:
                nc.scalar.activation(h[:], acc[:], COPY, scale=0.0625)
            else:
                nc.vector.tensor_scalar_mul(h[:], acc[:], 0.0625)
            return h

        def swap(i, h):
            pa = sb("pa%d" % i, [P, W], F32)
            pb = sb("pb%d" % i, [P, W], F32)
            rb = sb("rb%d" % i, [P, W], F32)
            dt = dts[i]
            nc.scalar.activation(pb[:], h[:].indirect(n2_l[:]), COPY)
            nc.scalar.activation(pa[:], h[:].indirect(n1_l[:]), COPY)
            nc.vector.tensor_tensor(rb[:], pa[:], pb[:], ALU.subtract)
            nc.scalar.activation(dt[:].indirect(n1_l[:]), pb[:], COPY)
            nc.scalar.activation(dt[:].indirect(n2_l[:]), rb[:], COPY)
            return dt

        def finish(i, dt, far_tag=None, res_tag=None):
            far = sb("far%d" % i, [P, S], F32, tag=far_tag)
            res = sb("res%d" % i, [P, S], F32, tag=res_tag)
            nc.scalar.activation(far[:], dt[:].indirect(n3_l[:]), COPY)
            nc.vector.scalar_tensor_tensor(res[:], far[:], 0.5, dt[:, 0:S], ALU.mult, ALU.max)
            nc.sync.dma_start(out[i * P : (i + 1) * P, :], res[:])

        hs = [product(i, words_a, plane_a, HALF) for i in range(2)]

        bytes_b = sb("bytes_b", [P, 2 * HALF], U8, tag="bytes_x")
        gather(bytes_b[:, 0:HALF], ds, k2_l, HALF, HALF)
        gather(bytes_b[:, HALF : 2 * HALF], ds, k1_l, HALF, HALF)
        place_scales(nc.sync, plane_b, bytes_b)
        dt0 = swap(0, hs[0])
        words_b = sb("words_b", [P, 2 * HALF], U32, tag="pa0")
        gather(words_b[:, 0:HALF], dw, k2_l, HALF, HALF)
        gather(words_b[:, HALF : 2 * HALF], dw, k1_l, HALF, HALF)
        dt1 = swap(1, hs[1])
        hs.extend([product(i, words_b, plane_b, 0) for i in range(2, 4)])
        dt2 = swap(2, hs[2])
        finish(0, dt0, res_tag="pa0")
        finish(1, dt1, far_tag="plane_b")
        dt3 = swap(3, hs[3])
        finish(2, dt2)
        far = sb("far3", [P, S], F32)
        res = sb("res3", [P, S], F32)
        for u in range(2):
            cols = slice(u * W, (u + 1) * W)
            nc.scalar.activation(far[:, cols], dt3[:].indirect(n3_l[:, 8 * u : 8 * (u + 1)]), COPY)
            nc.vector.scalar_tensor_tensor(res[:, cols], far[:, cols], 0.5, dt3[:, cols], ALU.mult, ALU.max)
            nc.sync.dma_start(out[3 * P : 4 * P, cols], res[:, cols])
